import numpy as np
import ml_dtypes


def mxq(x, axis, fmt="e4m3"):
    dtype, down = {"e4m3": (ml_dtypes.float8_e4m3fn, 7), "e5m2": (ml_dtypes.float8_e5m2, 14)}[fmt]
    v = np.moveaxis(np.asarray(x, np.float32).astype(ml_dtypes.bfloat16).astype(np.float64), axis, -1)
    blocks = v.reshape(v.shape[:-1] + (-1, 32))
    amax = np.abs(blocks).max(-1, keepdims=True)
    byte = np.maximum(np.where(amax > 0, np.frexp(amax)[1] - 1 + 127, 0) - down, 1)
    scale = np.exp2(byte - 127.0)
    codes = (blocks / scale).astype(np.float32).astype(dtype).astype(np.float64)
    return np.moveaxis((codes * scale).reshape(v.shape), -1, axis)


WIDE = False


def mx_kscale(k):
    if not WIDE:
        return np.ones(k)
    levels = np.array([30, -30])
    if k % 512:
        return np.exp2(np.random.permutation(np.resize(levels, k // 32))).repeat(32)
    a = np.empty((k // 512, 16))
    for p in range(k // 512):
        a[p, :8] = np.random.permutation(np.resize(levels, 8))
        for g in range(8):
            far = levels[np.abs(levels - a[p, g]) >= 10]
            a[p, g + 8] = far[np.random.randint(len(far))]
    return np.exp2(a.ravel()).repeat(32)


def f64(x):
    return np.asarray(x).astype(np.float64)


def striped(idx):
    return np.tile(np.asarray(idx).reshape(-1, 16).T, (8, 1)).astype(np.uint16)


def unstriped(offs):
    return offs[:16].T.reshape(-1).astype(np.int64)


E2M1 = np.array([0.0, 0.5, 1.0, 1.5, 2.0, 3.0, 4.0, 6.0, -0.0, -0.5, -1.0, -1.5, -2.0, -3.0, -4.0, -6.0])


def pack_weight(w, fmt):
    k, n = w.shape
    w = f64(np.asarray(w, np.float32).astype(ml_dtypes.bfloat16)).reshape(k // 32, 32, n)
    amax = np.abs(w).max(1)
    if fmt == "e4m3":
        byte = np.frexp(amax)[1] - 1 + 127 - 7
    else:
        mant, ex = np.frexp(amax / 6.0)
        byte = np.where(mant > 0.5, ex, ex - 1) + 127
    byte = np.clip(np.where(amax > 0, byte, 1), 1, 254)
    scaled = (w * np.exp2(127.0 - byte)[:, None, :]).reshape(k, n).astype(np.float32)
    by_word = np.ascontiguousarray(scaled.reshape(k // 512, 128, 4, n).transpose(0, 1, 3, 2))
    if fmt == "e4m3":
        words = by_word.astype(ml_dtypes.float8_e4m3fn).view(np.uint8)
    else:
        c = by_word.astype(ml_dtypes.float4_e2m1fn).view(np.uint8) & 0xF
        words = (c[..., 0::2] | (c[..., 1::2] << 4)).reshape(k // 512, 128, 2 * n)
    return np.ascontiguousarray(words), np.ascontiguousarray(byte.astype(np.uint8).reshape(k // 512, 16, n))


def unpack_weight(words, scales, fmt):
    g, _, n = scales.shape
    words = np.ascontiguousarray(words).reshape(g, 128, n, -1)
    if fmt == "e4m3":
        vals = words.view(ml_dtypes.float8_e4m3fn).astype(np.float64)
    else:
        nib = np.empty((g, 128, n, 4), np.uint8)
        nib[..., 0::2] = words & 0xF
        nib[..., 1::2] = words >> 4
        vals = E2M1[nib]
    vals = vals * np.repeat(np.exp2(scales.astype(np.float64) - 127.0), 8, axis=1)[..., None]
    return vals.transpose(0, 1, 3, 2).reshape(g * 512, n)


def sigmoid(v):
    return 1.0 / (1.0 + np.exp(-v))


K, T, Z, J, R, Q, N, L, E = 512, 1024, 1024, 256, 512, 1024, 256, 512, 1024


def setup_inputs():
    n = np.random.standard_normal
    idx = np.random.permutation(T)[:J]
    idx2 = np.random.permutation(Z)[:J]
    idx3 = np.random.permutation(Q)[:J]
    idx4 = np.random.permutation(E)[:J]
    fk = mx_kscale(K)
    fr = mx_kscale(R)
    fl = mx_kscale(L)
    xtp = pack_weight(n((K, T)) / fk[:, None], "e2m1")
    xop = pack_weight(n((K, Z)) / fk[:, None], "e4m3")
    wp = pack_weight(n((K, R)) * 1 / np.sqrt(K) * fk[:, None] * fr, "e4m3")
    wbp = pack_weight(n((R, N)) * 1 / np.sqrt(R) / fr[:, None], "e2m1")
    sxp = pack_weight(n((L, J)) / fl[:, None], "e4m3")
    wsp = pack_weight(n((L, N)) * 1 / np.sqrt(L) * fl[:, None], "e4m3")
    return {
        "xt_words": xtp[0],
        "xt_scales": xtp[1],
        "xo_words": xop[0],
        "xo_scales": xop[1],
        "w_words": wp[0],
        "w_scales": wp[1],
        "tg": (1.0 * n((R, Q))).astype(np.float32),
        "sg": (np.random.uniform(0.6, 1.6, (R, 1))).astype(np.float32),
        "bg": (np.random.uniform(-1.0, 1.0, (R, 1))).astype(np.float32),
        "wb_words": wbp[0],
        "wb_scales": wbp[1],
        "sx_words": sxp[0],
        "sx_scales": sxp[1],
        "ws_words": wsp[0],
        "ws_scales": wsp[1],
        "offs": striped(idx),
        "offs2": striped(idx2),
        "offs3": striped(idx3),
        "offs4": striped(idx4),
    }


def reference(xt_words, xt_scales, xo_words, xo_scales, w_words, w_scales, tg, sg, bg, wb_words, wb_scales, sx_words, sx_scales, ws_words, ws_scales, offs, offs2, offs3, offs4):
    idx = unstriped(offs)
    idx2 = unstriped(offs2)
    idx3 = unstriped(offs3)
    idx4 = unstriped(offs4)
    xtu = unpack_weight(xt_words, xt_scales, "e2m1")
    xou = unpack_weight(xo_words, xo_scales, "e4m3")
    wu = unpack_weight(w_words, w_scales, "e4m3")
    wbu = unpack_weight(wb_words, wb_scales, "e2m1")
    sxu = unpack_weight(sx_words, sx_scales, "e4m3")
    wsu = unpack_weight(ws_words, ws_scales, "e4m3")
    xtidxg = xtu[:, idx]
    a = wu.T @ xtidxg
    xoidx2g = xou[:, idx2]
    b = wu.T @ xoidx2g
    hid = np.maximum(a, b) * sigmoid(f64(tg)[:, idx3] * f64(sg) + f64(bg))
    hidq = mxq(hid, 0, "e5m2")
    p = wbu.T @ hidq + wsu.T @ sxu
    y = np.zeros((N, E))
    y[:, idx4] = p
    return y

@@ -1,0 +1,196 @@
+from contextlib import ExitStack
+
+import concourse.mybir as mybir
+
+K, T, Z, J, R, Q, N, L, E = 512, 1024, 1024, 256, 512, 1024, 256, 512, 1024
+FLOPS = 2 * (2 * K * R * J + R * N * J + L * N * J)
+
+F32 = mybir.dt.float32
+BF16 = mybir.dt.bfloat16
+I32 = mybir.dt.int32
+U32 = mybir.dt.uint32
+U16 = mybir.dt.uint16
+U8 = mybir.dt.uint8
+E4M3 = mybir.dt.float8_e4m3fn_x4
+E5M2 = mybir.dt.float8_e5m2_x4
+E2M1 = mybir.dt.float4_e2m1fn_x4
+ACT = mybir.ActivationFunctionType
+ALU = mybir.AluOpType
+
+P = 128
+PACK = 4
+ROWS = 16
+PARTS = 2
+JP = J // PARTS
+
+XT_S, XO_S, W_S, WB_S, SX_S, WS_S = 0, J, 2 * J, 2 * J + R, 2 * J + R + N, 3 * J + R + N
+W_RAW_S = WS_S + N
+PLANE_COLS = W_RAW_S + R
+
+
+def tile_list_oneforboth_tablegate_skip_scattered_kernel(
+    tc, xt_words, xt_scales, xo_words, xo_scales, w_words, w_scales, tg, sg, bg,
+    wb_words, wb_scales, sx_words, sx_scales, ws_words, ws_scales,
+    offs, offs2, offs3, offs4, out,
+):
+    nc = tc.nc
+    with ExitStack() as ctx:
+        keep = ctx.enter_context(tc.tile_pool(name="keep", bufs=1))
+        shared = ctx.enter_context(tc.tile_pool(name="shared", bufs=1))
+        psum = ctx.enter_context(tc.psum_pool(name="psum", bufs=1))
+
+        def sb(name, shape, dtype):
+            return keep.tile(shape, dtype, name=name, align_bytes=64)
+
+        token_list = sb("token_list", [P, J // 16], U16)
+        note_list = sb("note_list", [P, J // 16], U16)
+        gate_list = sb("gate_list", [P, J // 16], U16)
+        place_list = sb("place_list", [P, J // 16], U16)
+
+        xt_bytes = sb("xt_bytes", [P, T], U8)
+        xo_bytes = sb("xo_bytes", [P, Z], U8)
+        planes = sb("planes", [P, PLANE_COLS], U8)
+        xt_table = sb("xt_table", [P, T], U16)
+        xo_table = shared.tile([P, Z], U32, name="xo_table", align_bytes=64, offset=0)
+        w_raw = sb("w_raw", [P, R], U32)
+        w_codes = sb("w_codes", [P, R], U32)
+        xt_picked = sb("xt_picked", [P, J], U16)
+        xo_picked = sb("xo_picked", [P, J], U32)
+        xt_picked_bytes = sb("xt_picked_bytes", [P, J], U8)
+        xo_picked_bytes = sb("xo_picked_bytes", [P, J], U8)
+        slope = sb("slope", [P, PACK], F32)
+        offset = sb("offset", [P, PACK], F32)
+        gate_table = [sb(f"gate_table{t}", [P, Q], F32) for t in range(PACK)]
+        pages = [sb(f"page{h}", [P, E], F32) for h in range(N // P)]
+
+        nc.vector.memset(xt_bytes[:].bitcast(I32), 0)
+        nc.vector.memset(xo_bytes[:].bitcast(I32), 0)
+        nc.vector.memset(planes[:, WB_S:].bitcast(I32), 0)
+
+        def words(ap):
+            return ap[0].rearrange("p n t -> p (n t)").bitcast(I32)
+
+        def scale_rows(tile_cols, src):
+            nc.sync.dma_start(tile_cols.bitcast(I32), src[0].bitcast(I32))
+
+        nc.sync.dma_start(token_list[:], offs)
+        nc.sync.dma_start(note_list[:], offs2)
+        nc.sync.dma_start(xt_table[:].bitcast(I32), xt_words[0].bitcast(I32))
+        scale_rows(xt_bytes[0:ROWS, :], xt_scales)
+        scale_rows(xo_bytes[0:ROWS, :], xo_scales)
+        scale_rows(planes[0:ROWS, W_RAW_S : W_RAW_S + R], w_scales)
+        scale_rows(planes[0:ROWS, WB_S : WB_S + N], wb_scales)
+        nc.sync.dma_start(xo_table[:].bitcast(I32), words(xo_words))
+        nc.sync.dma_start(w_raw[:].bitcast(I32), words(w_words))
+        scale_rows(planes[0:ROWS, SX_S : SX_S + J], sx_scales)
+        scale_rows(planes[0:ROWS, WS_S : WS_S + N], ws_scales)
+        nc.sync.dma_start(gate_list[:], offs3)
+        tg_rows = tg.rearrange("(p t) q -> t p q", t=PACK)
+        for t in range(PACK):
+            nc.sync.dma_start(gate_table[t][:], tg_rows[t])
+        nc.sync.dma_start(place_list[:], offs4)
+        nc.gpsimd.dma_start(slope[:], sg.rearrange("(p t) o -> p (t o)", t=PACK))
+        nc.gpsimd.dma_start(offset[:], bg.rearrange("(p t) o -> p (t o)", t=PACK))
+
+        for page in pages:
+            nc.vector.memset(page[:], 0.0)
+
+        nc.vector.tensor_copy(xt_picked_bytes[:], xt_bytes[:].indirect(token_list[:]))
+        nc.vector.tensor_copy(xo_picked_bytes[:], xo_bytes[:].indirect(note_list[:]))
+        nc.vector.tensor_copy(
+            planes[:, W_S : W_S + R].rearrange("p (t m) -> p t m", t=PACK),
+            planes[:, W_RAW_S:].rearrange("p (m t) -> p t m", t=PACK),
+        )
+        nc.vector.tensor_copy(planes[:, XT_S : XT_S + J].bitcast(I32), xt_picked_bytes[:].bitcast(I32))
+        nc.vector.tensor_copy(planes[:, XO_S : XO_S + J].bitcast(I32), xo_picked_bytes[:].bitcast(I32))
+        for quad in range(1, 4):
+            nc.scalar.dma_start(
+                planes[32 * quad : 32 * quad + 4, :W_RAW_S].bitcast(I32),
+                planes[4 * quad : 4 * quad + 4, :W_RAW_S].bitcast(I32),
+            )
+
+        nc.vector.tensor_copy(xt_picked[:], xt_table[:].indirect(token_list[:]))
+        nc.vector.tensor_copy(xo_picked[:], xo_table[:].indirect(note_list[:]))
+        nc.vector.tensor_copy(
+            w_codes[:].rearrange("p (t m) -> p m t", t=PACK),
+            w_raw[:].rearrange("p (m t) -> p m t", t=PACK),
+        )
+
+        ws_codes = shared.tile([P, N], U32, name="ws_codes", align_bytes=64, offset=0)
+        sx_codes = shared.tile([P, J], U32, name="sx_codes", align_bytes=64, offset=4 * N)
+        wb_codes = shared.tile([P, 2 * N], U8, name="wb_codes", align_bytes=64, offset=4 * N + 4 * J)
+        nc.sync.dma_start(ws_codes[:].bitcast(I32), words(ws_words))
+        nc.sync.dma_start(sx_codes[:].bitcast(I32), words(sx_words))
+        nc.sync.dma_start(wb_codes[:].bitcast(I32), wb_words[0].bitcast(I32))
+
+        gates = [sb(f"gates{u}", [P, 2, J], F32) for u in range(2)]
+        larger = [sb(f"larger{u}", [P, 2, J], F32) for u in range(2)]
+        hid = [sb(f"hid{c}", [P, JP, PACK], BF16) for c in range(PARTS)]
+        for u in range(2):
+            for e in range(2):
+                t = 2 * u + e
+                nc.scalar.activation(
+                    out=gates[u][:, e, :], in_=gate_table[t][:].indirect(gate_list[:]),
+                    func=ACT.Sigmoid, bias=offset[:, t : t + 1], scale=slope[:, t : t + 1],
+                )
+                both = psum.tile([P, 2, J], F32, name=f"both{t}")
+                cols = slice(t * P, (t + 1) * P)
+                w_plane = planes[:, W_S + t * P : W_S + (t + 1) * P]
+                nc.tensor.matmul_mx(
+                    out=both[:, 0, :], lhsT=w_codes[:, cols].bitcast(E4M3), lhsT_scale=w_plane,
+                    rhs=xt_picked[:].bitcast(E2M1), rhs_scale=planes[:, XT_S : XT_S + J],
+                    start=True, stop=True,
+                )
+                nc.tensor.matmul_mx(
+                    out=both[:, 1, :], lhsT=w_codes[:, cols].bitcast(E4M3), lhsT_scale=w_plane,
+                    rhs=xo_picked[:].bitcast(E4M3), rhs_scale=planes[:, XO_S : XO_S + J],
+                    start=True, stop=True,
+                )
+                nc.vector.tensor_reduce(
+                    larger[u][:, e, :], both[:].rearrange("p s j -> p j s"), mybir.AxisListType.X, ALU.max
+                )
+            for c in range(PARTS):
+                js = slice(c * JP, (c + 1) * JP)
+                nc.vector.tensor_tensor(
+                    hid[c][:, :, 2 * u : 2 * u + 2],
+                    larger[u][:, :, js].rearrange("p e j -> p j e"),
+                    gates[u][:, :, js].rearrange("p e j -> p j e"),
+                    ALU.mult,
+                )
+
+        hid_codes = [sb(f"hid_codes{c}", [P, JP], U32) for c in range(PARTS)]
+        hid_plane = [sb(f"hid_plane{c}", [P, JP], U8) for c in range(PARTS)]
+        for c in range(PARTS):
+            nc.vector.quantize_mx(
+                out=hid_codes[c][:].bitcast(E5M2), scales=hid_plane[c][:],
+                in_=hid[c][:].rearrange("p j t -> p (j t)"),
+            )
+
+        for c in range(PARTS):
+            js = slice(c * JP, (c + 1) * JP)
+            places = place_list[:, c * JP // 16 : (c + 1) * JP // 16]
+            for h in range(N // P):
+                acc = psum.tile([P, JP], F32, name=f"acc{c}_{h}")
+                nc.tensor.matmul_mx(
+                    out=acc[:], lhsT=ws_codes[:, h * P : (h + 1) * P].bitcast(E4M3),
+                    lhsT_scale=planes[:, WS_S + h * P : WS_S + (h + 1) * P],
+                    rhs=sx_codes[:, js].bitcast(E4M3),
+                    rhs_scale=planes[:, SX_S + c * JP : SX_S + (c + 1) * JP],
+                    start=True, stop=False,
+                )
+                nc.tensor.matmul_mx(
+                    out=acc[:], lhsT=wb_codes[:, 2 * h * P : 2 * (h + 1) * P].bitcast(E2M1),
+                    lhsT_scale=planes[:, WB_S + h * P : WB_S + (h + 1) * P],
+                    rhs=hid_codes[c][:].bitcast(E5M2), rhs_scale=hid_plane[c][:],
+                    start=False, stop=True,
+                )
+                result = sb(f"result{c}_{h}", [P, JP], F32)
+                if h == 0:
+                    nc.vector.tensor_copy(result[:], acc[:])
+                    nc.vector.tensor_copy(pages[h][:].indirect(places), result[:])
+                else:
+                    nc.scalar.copy(result[:], acc[:])
+                    nc.scalar.activation(out=pages[h][:].indirect(places), in_=result[:], func=ACT.Copy)
+
+        nc.sync.dma_start(out[0:P, :], pages[0][:])
+        nc.scalar.dma_start(out[P : 2 * P, :], pages[1][:])

@@ -20,6 +20,7 @@ ALU = mybir.AluOpType
 P = 128
 PACK = 4
 ROWS = 16
+LOW = P - ROWS
 PARTS = 2
 JP = J // PARTS
 
@@ -42,6 +43,9 @@ def tile_list_oneforboth_tablegate_skip_scattered_kernel(
         def sb(name, shape, dtype):
             return keep.tile(shape, dtype, name=name, align_bytes=64)
 
+        def placed(name, shape, dtype, byte):
+            return shared.tile(shape, dtype, name=name, align_bytes=64, offset=byte)
+
         token_list = sb("token_list", [P, J // 16], U16)
         note_list = sb("note_list", [P, J // 16], U16)
         gate_list = sb("gate_list", [P, J // 16], U16)
@@ -50,9 +54,9 @@ def tile_list_oneforboth_tablegate_skip_scattered_kernel(
         xt_bytes = sb("xt_bytes", [P, T], U8)
         xo_bytes = sb("xo_bytes", [P, Z], U8)
         planes = sb("planes", [P, PLANE_COLS], U8)
-        xt_table = sb("xt_table", [P, T], U16)
-        xo_table = shared.tile([P, Z], U32, name="xo_table", align_bytes=64, offset=0)
-        w_raw = sb("w_raw", [P, R], U32)
+        xt_table = placed("xt_table", [P, T], U16, 3 * 4 * Q)
+        xo_table = placed("xo_table", [P, Z], U32, 4 * Q + 2 * Q)
+        w_raw = placed("w_raw", [P, R], U32, 4 * 4 * Q)
         w_codes = sb("w_codes", [P, R], U32)
         xt_picked = sb("xt_picked", [P, J], U16)
         xo_picked = sb("xo_picked", [P, J], U32)
@@ -60,12 +64,11 @@ def tile_list_oneforboth_tablegate_skip_scattered_kernel(
         xo_picked_bytes = sb("xo_picked_bytes", [P, J], U8)
         slope = sb("slope", [P, PACK], F32)
         offset = sb("offset", [P, PACK], F32)
-        gate_table = [sb(f"gate_table{t}", [P, Q], F32) for t in range(PACK)]
-        pages = [sb(f"page{h}", [P, E], F32) for h in range(N // P)]
+        gate_table = [placed("gate_table0", [P, Q], F32, 0), sb("gate_table1", [P, Q], F32)]
 
-        nc.vector.memset(xt_bytes[:].bitcast(I32), 0)
-        nc.vector.memset(xo_bytes[:].bitcast(I32), 0)
-        nc.vector.memset(planes[:, WB_S:].bitcast(I32), 0)
+        nc.vector.memset(xt_bytes[:LOW, :].bitcast(I32), 0)
+        nc.vector.memset(xo_bytes[:LOW, :].bitcast(I32), 0)
+        nc.vector.memset(planes[:LOW, WB_S:].bitcast(I32), 0)
 
         def words(ap):
             return ap[0].rearrange("p n t -> p (n t)").bitcast(I32)
@@ -75,25 +78,22 @@ def tile_list_oneforboth_tablegate_skip_scattered_kernel(
 
         nc.sync.dma_start(token_list[:], offs)
         nc.sync.dma_start(note_list[:], offs2)
-        nc.sync.dma_start(xt_table[:].bitcast(I32), xt_words[0].bitcast(I32))
-        scale_rows(xt_bytes[0:ROWS, :], xt_scales)
-        scale_rows(xo_bytes[0:ROWS, :], xo_scales)
-        scale_rows(planes[0:ROWS, W_RAW_S : W_RAW_S + R], w_scales)
-        scale_rows(planes[0:ROWS, WB_S : WB_S + N], wb_scales)
+        scale_rows(xt_bytes[LOW:, :], xt_scales)
+        scale_rows(xo_bytes[LOW:, :], xo_scales)
+        scale_rows(planes[LOW:, W_RAW_S : W_RAW_S + R], w_scales)
+        scale_rows(planes[LOW:, WB_S : WB_S + N], wb_scales)
         nc.sync.dma_start(xo_table[:].bitcast(I32), words(xo_words))
-        nc.sync.dma_start(w_raw[:].bitcast(I32), words(w_words))
-        scale_rows(planes[0:ROWS, SX_S : SX_S + J], sx_scales)
-        scale_rows(planes[0:ROWS, WS_S : WS_S + N], ws_scales)
+        nc.sync.dma_start(xt_table[:].bitcast(I32), xt_words[0].bitcast(I32))
+        scale_rows(planes[LOW:, SX_S : SX_S + J], sx_scales)
+        scale_rows(planes[LOW:, WS_S : WS_S + N], ws_scales)
         nc.sync.dma_start(gate_list[:], offs3)
-        tg_rows = tg.rearrange("(p t) q -> t p q", t=PACK)
-        for t in range(PACK):
-            nc.sync.dma_start(gate_table[t][:], tg_rows[t])
         nc.sync.dma_start(place_list[:], offs4)
+        nc.sync.dma_start(w_raw[:].bitcast(I32), words(w_words))
+        tg_rows = tg.rearrange("(p t) q -> t p q", t=PACK)
+        for t in range(2):
+            nc.sync.dma_start(gate_table[t][:], tg_rows[t])
         nc.gpsimd.dma_start(slope[:], sg.rearrange("(p t) o -> p (t o)", t=PACK))
         nc.gpsimd.dma_start(offset[:], bg.rearrange("(p t) o -> p (t o)", t=PACK))
-
-        for page in pages:
-            nc.vector.memset(page[:], 0.0)
 
         nc.vector.tensor_copy(xt_picked_bytes[:], xt_bytes[:].indirect(token_list[:]))
         nc.vector.tensor_copy(xo_picked_bytes[:], xo_bytes[:].indirect(note_list[:]))
@@ -103,25 +103,26 @@ def tile_list_oneforboth_tablegate_skip_scattered_kernel(
         )
         nc.vector.tensor_copy(planes[:, XT_S : XT_S + J].bitcast(I32), xt_picked_bytes[:].bitcast(I32))
         nc.vector.tensor_copy(planes[:, XO_S : XO_S + J].bitcast(I32), xo_picked_bytes[:].bitcast(I32))
-        for quad in range(1, 4):
+        for quad in range(4):
             nc.scalar.dma_start(
                 planes[32 * quad : 32 * quad + 4, :W_RAW_S].bitcast(I32),
-                planes[4 * quad : 4 * quad + 4, :W_RAW_S].bitcast(I32),
+                planes[LOW + 4 * quad : LOW + 4 * quad + 4, :W_RAW_S].bitcast(I32),
             )
 
-        nc.vector.tensor_copy(xt_picked[:], xt_table[:].indirect(token_list[:]))
         nc.vector.tensor_copy(xo_picked[:], xo_table[:].indirect(note_list[:]))
+        for t in range(2, PACK):
+            gate_table.append(placed(f"gate_table{t}", [P, Q], F32, (t - 1) * 4 * Q))
+            nc.sync.dma_start(gate_table[t][:], tg_rows[t])
+
+        nc.vector.tensor_copy(xt_picked[:], xt_table[:].indirect(token_list[:]))
         nc.vector.tensor_copy(
             w_codes[:].rearrange("p (t m) -> p m t", t=PACK),
             w_raw[:].rearrange("p (m t) -> p m t", t=PACK),
         )
 
-        ws_codes = shared.tile([P, N], U32, name="ws_codes", align_bytes=64, offset=0)
-        sx_codes = shared.tile([P, J], U32, name="sx_codes", align_bytes=64, offset=4 * N)
-        wb_codes = shared.tile([P, 2 * N], U8, name="wb_codes", align_bytes=64, offset=4 * N + 4 * J)
-        nc.sync.dma_start(ws_codes[:].bitcast(I32), words(ws_words))
-        nc.sync.dma_start(sx_codes[:].bitcast(I32), words(sx_words))
-        nc.sync.dma_start(wb_codes[:].bitcast(I32), wb_words[0].bitcast(I32))
+        pages = [placed(f"page{h}", [P, E], F32, (3 + h) * 4 * Q) for h in range(N // P)]
+        for page in pages:
+            nc.vector.memset(page[:], 0.0)
 
         gates = [sb(f"gates{u}", [P, 2, J], F32) for u in range(2)]
         larger = [sb(f"larger{u}", [P, 2, J], F32) for u in range(2)]
@@ -158,6 +159,26 @@ def tile_list_oneforboth_tablegate_skip_scattered_kernel(
                     ALU.mult,
                 )
 
+        ws_codes = shared.tile([P, N], U32, name="ws_codes", align_bytes=64, offset=0)
+        sx_codes = shared.tile([P, J], U32, name="sx_codes", align_bytes=64, offset=4 * N)
+        wb_codes = shared.tile([P, 2 * N], U8, name="wb_codes", align_bytes=64, offset=4 * N + 4 * J)
+        nc.sync.dma_start(ws_codes[:].bitcast(I32), words(ws_words))
+        nc.sync.dma_start(sx_codes[:].bitcast(I32), words(sx_words))
+        nc.sync.dma_start(wb_codes[:].bitcast(I32), wb_words[0].bitcast(I32))
+
+        sums = {}
+        for c in range(PARTS):
+            js = slice(c * JP, (c + 1) * JP)
+            for h in range(N // P):
+                sums[c, h] = psum.tile([P, JP], F32, name=f"sum{c}_{h}")
+                nc.tensor.matmul_mx(
+                    out=sums[c, h][:], lhsT=ws_codes[:, h * P : (h + 1) * P].bitcast(E4M3),
+                    lhsT_scale=planes[:, WS_S + h * P : WS_S + (h + 1) * P],
+                    rhs=sx_codes[:, js].bitcast(E4M3),
+                    rhs_scale=planes[:, SX_S + c * JP : SX_S + (c + 1) * JP],
+                    start=True, stop=False,
+                )
+
         hid_codes = [sb(f"hid_codes{c}", [P, JP], U32) for c in range(PARTS)]
         hid_plane = [sb(f"hid_plane{c}", [P, JP], U8) for c in range(PARTS)]
         for c in range(PARTS):
@@ -167,29 +188,20 @@ def tile_list_oneforboth_tablegate_skip_scattered_kernel(
             )
 
         for c in range(PARTS):
-            js = slice(c * JP, (c + 1) * JP)
             places = place_list[:, c * JP // 16 : (c + 1) * JP // 16]
             for h in range(N // P):
-                acc = psum.tile([P, JP], F32, name=f"acc{c}_{h}")
                 nc.tensor.matmul_mx(
-                    out=acc[:], lhsT=ws_codes[:, h * P : (h + 1) * P].bitcast(E4M3),
-                    lhsT_scale=planes[:, WS_S + h * P : WS_S + (h + 1) * P],
-                    rhs=sx_codes[:, js].bitcast(E4M3),
-                    rhs_scale=planes[:, SX_S + c * JP : SX_S + (c + 1) * JP],
-                    start=True, stop=False,
-                )
-                nc.tensor.matmul_mx(
-                    out=acc[:], lhsT=wb_codes[:, 2 * h * P : 2 * (h + 1) * P].bitcast(E2M1),
+                    out=sums[c, h][:], lhsT=wb_codes[:, 2 * h * P : 2 * (h + 1) * P].bitcast(E2M1),
                     lhsT_scale=planes[:, WB_S + h * P : WB_S + (h + 1) * P],
                     rhs=hid_codes[c][:].bitcast(E5M2), rhs_scale=hid_plane[c][:],
                     start=False, stop=True,
                 )
                 result = sb(f"result{c}_{h}", [P, JP], F32)
                 if h == 0:
-                    nc.vector.tensor_copy(result[:], acc[:])
+                    nc.vector.tensor_copy(result[:], sums[c, h][:])
                     nc.vector.tensor_copy(pages[h][:].indirect(places), result[:])
                 else:
-                    nc.scalar.copy(result[:], acc[:])
+                    nc.scalar.copy(result[:], sums[c, h][:])
                     nc.scalar.activation(out=pages[h][:].indirect(places), in_=result[:], func=ACT.Copy)
 
         nc.sync.dma_start(out[0:P, :], pages[0][:])

@@ -54,17 +54,17 @@ def tile_list_oneforboth_tablegate_skip_scattered_kernel(
         xt_bytes = sb("xt_bytes", [P, T], U8)
         xo_bytes = sb("xo_bytes", [P, Z], U8)
         planes = sb("planes", [P, PLANE_COLS], U8)
-        xt_table = placed("xt_table", [P, T], U16, 3 * 4 * Q)
-        xo_table = placed("xo_table", [P, Z], U32, 4 * Q + 2 * Q)
-        w_raw = placed("w_raw", [P, R], U32, 4 * 4 * Q)
+        xt_table = placed("xt_table", [P, T], U16, 12800)
+        xo_table = placed("xo_table", [P, Z], U32, 6144)
+        w_raw = placed("w_raw", [P, R], U32, 14848)
         w_codes = sb("w_codes", [P, R], U32)
         xt_picked = sb("xt_picked", [P, J], U16)
         xo_picked = sb("xo_picked", [P, J], U32)
         xt_picked_bytes = sb("xt_picked_bytes", [P, J], U8)
-        xo_picked_bytes = sb("xo_picked_bytes", [P, J], U8)
+        xo_picked_bytes = placed("xo_picked_bytes", [P, J], U8, 0)
         slope = sb("slope", [P, PACK], F32)
         offset = sb("offset", [P, PACK], F32)
-        gate_table = [placed("gate_table0", [P, Q], F32, 0), sb("gate_table1", [P, Q], F32)]
+        gate_table = [sb("gate_table0", [P, Q], F32)]
 
         nc.vector.memset(xt_bytes[:LOW, :].bitcast(I32), 0)
         nc.vector.memset(xo_bytes[:LOW, :].bitcast(I32), 0)
@@ -90,10 +90,9 @@ def tile_list_oneforboth_tablegate_skip_scattered_kernel(
         nc.sync.dma_start(place_list[:], offs4)
         nc.sync.dma_start(w_raw[:].bitcast(I32), words(w_words))
         tg_rows = tg.rearrange("(p t) q -> t p q", t=PACK)
-        for t in range(2):
-            nc.sync.dma_start(gate_table[t][:], tg_rows[t])
-        nc.gpsimd.dma_start(slope[:], sg.rearrange("(p t) o -> p (t o)", t=PACK))
-        nc.gpsimd.dma_start(offset[:], bg.rearrange("(p t) o -> p (t o)", t=PACK))
+        nc.sync.dma_start(gate_table[0][:], tg_rows[0])
+        nc.sync.dma_start(slope[:], sg.rearrange("(p t) o -> p (t o)", t=PACK))
+        nc.sync.dma_start(offset[:], bg.rearrange("(p t) o -> p (t o)", t=PACK))
 
         nc.vector.tensor_copy(xt_picked_bytes[:], xt_bytes[:].indirect(token_list[:]))
         nc.vector.tensor_copy(xo_picked_bytes[:], xo_bytes[:].indirect(note_list[:]))
@@ -104,23 +103,30 @@ def tile_list_oneforboth_tablegate_skip_scattered_kernel(
         nc.vector.tensor_copy(planes[:, XT_S : XT_S + J].bitcast(I32), xt_picked_bytes[:].bitcast(I32))
         nc.vector.tensor_copy(planes[:, XO_S : XO_S + J].bitcast(I32), xo_picked_bytes[:].bitcast(I32))
         for quad in range(4):
-            nc.scalar.dma_start(
+            nc.sync.dma_start(
                 planes[32 * quad : 32 * quad + 4, :W_RAW_S].bitcast(I32),
                 planes[LOW + 4 * quad : LOW + 4 * quad + 4, :W_RAW_S].bitcast(I32),
             )
 
         nc.vector.tensor_copy(xo_picked[:], xo_table[:].indirect(note_list[:]))
-        for t in range(2, PACK):
-            gate_table.append(placed(f"gate_table{t}", [P, Q], F32, (t - 1) * 4 * Q))
+        for t in range(1, PACK):
+            gate_table.append(placed(f"gate_table{t}", [P, Q], F32, (0, 4096, 8704)[t - 1]))
             nc.sync.dma_start(gate_table[t][:], tg_rows[t])
 
         nc.vector.tensor_copy(xt_picked[:], xt_table[:].indirect(token_list[:]))
         nc.vector.tensor_copy(
-            w_codes[:].rearrange("p (t m) -> p m t", t=PACK),
-            w_raw[:].rearrange("p (m t) -> p m t", t=PACK),
+            w_codes[:].rearrange("p (t m) -> p t m", t=PACK),
+            w_raw[:].rearrange("p (m t) -> p t m", t=PACK),
         )
 
-        pages = [placed(f"page{h}", [P, E], F32, (3 + h) * 4 * Q) for h in range(N // P)]
+        ws_codes = placed("ws_codes", [P, N], U32, 12800)
+        sx_codes = placed("sx_codes", [P, J], U32, 12800 + 1024)
+        wb_codes = placed("wb_codes", [P, 2 * N], U8, 8192)
+        nc.sync.dma_start(ws_codes[:].bitcast(I32), words(ws_words))
+        nc.sync.dma_start(sx_codes[:].bitcast(I32), words(sx_words))
+        nc.sync.dma_start(wb_codes[:].bitcast(I32), wb_words[0].bitcast(I32))
+
+        pages = [sb("page0", [P, E], F32), placed("page1", [P, E], F32, 14848)]
         for page in pages:
             nc.vector.memset(page[:], 0.0)
 
@@ -150,6 +156,7 @@ def tile_list_oneforboth_tablegate_skip_scattered_kernel(
                 nc.vector.tensor_reduce(
                     larger[u][:, e, :], both[:].rearrange("p s j -> p j s"), mybir.AxisListType.X, ALU.max
                 )
+        for u in range(2):
             for c in range(PARTS):
                 js = slice(c * JP, (c + 1) * JP)
                 nc.vector.tensor_tensor(
@@ -158,13 +165,6 @@ def tile_list_oneforboth_tablegate_skip_scattered_kernel(
                     gates[u][:, :, js].rearrange("p e j -> p j e"),
                     ALU.mult,
                 )
-
-        ws_codes = shared.tile([P, N], U32, name="ws_codes", align_bytes=64, offset=0)
-        sx_codes = shared.tile([P, J], U32, name="sx_codes", align_bytes=64, offset=4 * N)
-        wb_codes = shared.tile([P, 2 * N], U8, name="wb_codes", align_bytes=64, offset=4 * N + 4 * J)
-        nc.sync.dma_start(ws_codes[:].bitcast(I32), words(ws_words))
-        nc.sync.dma_start(sx_codes[:].bitcast(I32), words(sx_words))
-        nc.sync.dma_start(wb_codes[:].bitcast(I32), wb_words[0].bitcast(I32))
 
         sums = {}
         for c in range(PARTS):

@@ -19,14 +19,29 @@ ALU = mybir.AluOpType
 
 P = 128
 PACK = 4
+GROUP = 16
+QUADS = 4
 ROWS = 16
 LOW = P - ROWS
-PARTS = 2
-JP = J // PARTS
+HALVES = 2
+JH = J // HALVES
 
-XT_S, XO_S, W_S, WB_S, SX_S, WS_S = 0, J, 2 * J, 2 * J + R, 2 * J + R + N, 3 * J + R + N
-W_RAW_S = WS_S + N
-PLANE_COLS = W_RAW_S + R
+XT_S, XO_S, W_S = 0, J, 2 * J
+WB_S = W_S + R
+SX_S = WB_S + N
+WS_S = SX_S + J
+W_RAW = WS_S + N
+PLANE_COLS = W_RAW + R
+
+TABLE_BYTES = 4 * Q
+GATE1_AT = 0
+GATE2_AT = GATE1_AT + TABLE_BYTES
+WB_AT = GATE2_AT + TABLE_BYTES
+GATE3_AT = WB_AT + 2 * N
+XO_TABLE_AT = WB_AT - 4 * Z // 2
+XT_TABLE_AT = GATE3_AT + TABLE_BYTES
+PAGES_AT = XT_TABLE_AT + 2 * T
+W_WORDS_AT = PAGES_AT + 4 * E - 4 * R // 2
 
 
 def tile_list_oneforboth_tablegate_skip_scattered_kernel(
@@ -46,22 +61,28 @@ def tile_list_oneforboth_tablegate_skip_scattered_kernel(
         def placed(name, shape, dtype, byte):
             return shared.tile(shape, dtype, name=name, align_bytes=64, offset=byte)
 
-        token_list = sb("token_list", [P, J // 16], U16)
-        note_list = sb("note_list", [P, J // 16], U16)
-        gate_list = sb("gate_list", [P, J // 16], U16)
-        place_list = sb("place_list", [P, J // 16], U16)
+        def words(ap):
+            return ap[0].rearrange("p n t -> p (n t)").bitcast(I32)
+
+        def load_scale_rows(queue, tile, first, src):
+            queue.dma_start(tile[LOW:, first : first + src.shape[2]].bitcast(I32), src[0].bitcast(I32))
+
+        token_list = sb("token_list", [P, J // GROUP], U16)
+        note_list = sb("note_list", [P, J // GROUP], U16)
+        gate_list = sb("gate_list", [P, J // GROUP], U16)
+        place_list = sb("place_list", [P, J // GROUP], U16)
 
         xt_bytes = sb("xt_bytes", [P, T], U8)
         xo_bytes = sb("xo_bytes", [P, Z], U8)
         planes = sb("planes", [P, PLANE_COLS], U8)
-        xt_table = placed("xt_table", [P, T], U16, 12800)
-        xo_table = placed("xo_table", [P, Z], U32, 6144)
-        w_raw = placed("w_raw", [P, R], U32, 14848)
+        xt_table = placed("xt_table", [P, T], U16, XT_TABLE_AT)
+        xo_table = placed("xo_table", [P, Z], U32, XO_TABLE_AT)
+        w_raw = placed("w_raw", [P, R], U32, W_WORDS_AT)
         w_codes = sb("w_codes", [P, R], U32)
         xt_picked = sb("xt_picked", [P, J], U16)
         xo_picked = sb("xo_picked", [P, J], U32)
         xt_picked_bytes = sb("xt_picked_bytes", [P, J], U8)
-        xo_picked_bytes = placed("xo_picked_bytes", [P, J], U8, 0)
+        xo_picked_bytes = placed("xo_picked_bytes", [P, J], U8, GATE1_AT)
         slope = sb("slope", [P, PACK], F32)
         offset = sb("offset", [P, PACK], F32)
         gate_table = [sb("gate_table0", [P, Q], F32)]
@@ -70,48 +91,43 @@ def tile_list_oneforboth_tablegate_skip_scattered_kernel(
         nc.vector.memset(xo_bytes[:LOW, :].bitcast(I32), 0)
         nc.vector.memset(planes[:LOW, WB_S:].bitcast(I32), 0)
 
-        def words(ap):
-            return ap[0].rearrange("p n t -> p (n t)").bitcast(I32)
-
-        def scale_rows(tile_cols, src):
-            nc.sync.dma_start(tile_cols.bitcast(I32), src[0].bitcast(I32))
-
+        load_scale_rows(nc.scalar, planes, W_RAW, w_scales)
+        load_scale_rows(nc.scalar, planes, WB_S, wb_scales)
         nc.sync.dma_start(token_list[:], offs)
+        load_scale_rows(nc.sync, xt_bytes, 0, xt_scales)
         nc.sync.dma_start(note_list[:], offs2)
-        scale_rows(xt_bytes[LOW:, :], xt_scales)
-        scale_rows(xo_bytes[LOW:, :], xo_scales)
-        scale_rows(planes[LOW:, W_RAW_S : W_RAW_S + R], w_scales)
-        scale_rows(planes[LOW:, WB_S : WB_S + N], wb_scales)
+        load_scale_rows(nc.sync, xo_bytes, 0, xo_scales)
         nc.sync.dma_start(xo_table[:].bitcast(I32), words(xo_words))
         nc.sync.dma_start(xt_table[:].bitcast(I32), xt_words[0].bitcast(I32))
-        scale_rows(planes[LOW:, SX_S : SX_S + J], sx_scales)
-        scale_rows(planes[LOW:, WS_S : WS_S + N], ws_scales)
+        load_scale_rows(nc.sync, planes, SX_S, sx_scales)
+        load_scale_rows(nc.sync, planes, WS_S, ws_scales)
         nc.sync.dma_start(gate_list[:], offs3)
         nc.sync.dma_start(place_list[:], offs4)
         nc.sync.dma_start(w_raw[:].bitcast(I32), words(w_words))
-        tg_rows = tg.rearrange("(p t) q -> t p q", t=PACK)
-        nc.sync.dma_start(gate_table[0][:], tg_rows[0])
+        tg_slices = tg.rearrange("(p t) q -> t p q", t=PACK)
+        nc.sync.dma_start(gate_table[0][:], tg_slices[0])
         nc.sync.dma_start(slope[:], sg.rearrange("(p t) o -> p (t o)", t=PACK))
         nc.sync.dma_start(offset[:], bg.rearrange("(p t) o -> p (t o)", t=PACK))
 
-        nc.vector.tensor_copy(xt_picked_bytes[:], xt_bytes[:].indirect(token_list[:]))
-        nc.vector.tensor_copy(xo_picked_bytes[:], xo_bytes[:].indirect(note_list[:]))
         nc.vector.tensor_copy(
             planes[:, W_S : W_S + R].rearrange("p (t m) -> p t m", t=PACK),
-            planes[:, W_RAW_S:].rearrange("p (m t) -> p t m", t=PACK),
+            planes[:, W_RAW:].rearrange("p (m t) -> p t m", t=PACK),
         )
+        nc.vector.tensor_copy(xt_picked_bytes[:], xt_bytes[:].indirect(token_list[:]))
+        nc.vector.tensor_copy(xo_picked_bytes[:], xo_bytes[:].indirect(note_list[:]))
         nc.vector.tensor_copy(planes[:, XT_S : XT_S + J].bitcast(I32), xt_picked_bytes[:].bitcast(I32))
         nc.vector.tensor_copy(planes[:, XO_S : XO_S + J].bitcast(I32), xo_picked_bytes[:].bitcast(I32))
-        for quad in range(4):
+
+        for quad in range(QUADS):
             nc.sync.dma_start(
-                planes[32 * quad : 32 * quad + 4, :W_RAW_S].bitcast(I32),
-                planes[LOW + 4 * quad : LOW + 4 * quad + 4, :W_RAW_S].bitcast(I32),
+                planes[32 * quad : 32 * quad + 4, :W_RAW].bitcast(I32),
+                planes[LOW + 4 * quad : LOW + 4 * quad + 4, :W_RAW].bitcast(I32),
             )
 
         nc.vector.tensor_copy(xo_picked[:], xo_table[:].indirect(note_list[:]))
-        for t in range(1, PACK):
-            gate_table.append(placed(f"gate_table{t}", [P, Q], F32, (0, 4096, 8704)[t - 1]))
-            nc.sync.dma_start(gate_table[t][:], tg_rows[t])
+        for t, byte in ((1, GATE1_AT), (2, GATE2_AT), (3, GATE3_AT)):
+            gate_table.append(placed(f"gate_table{t}", [P, Q], F32, byte))
+            nc.sync.dma_start(gate_table[t][:], tg_slices[t])
 
         nc.vector.tensor_copy(xt_picked[:], xt_table[:].indirect(token_list[:]))
         nc.vector.tensor_copy(
@@ -119,46 +135,46 @@ def tile_list_oneforboth_tablegate_skip_scattered_kernel(
             w_raw[:].rearrange("p (m t) -> p t m", t=PACK),
         )
 
-        ws_codes = placed("ws_codes", [P, N], U32, 12800)
-        sx_codes = placed("sx_codes", [P, J], U32, 12800 + 1024)
-        wb_codes = placed("wb_codes", [P, 2 * N], U8, 8192)
+        ws_codes = placed("ws_codes", [P, N], U32, XT_TABLE_AT)
+        sx_codes = placed("sx_codes", [P, J], U32, XT_TABLE_AT + 4 * N)
+        wb_codes = placed("wb_codes", [P, 2 * N], U8, WB_AT)
         nc.sync.dma_start(ws_codes[:].bitcast(I32), words(ws_words))
         nc.sync.dma_start(sx_codes[:].bitcast(I32), words(sx_words))
         nc.sync.dma_start(wb_codes[:].bitcast(I32), wb_words[0].bitcast(I32))
 
-        pages = [sb("page0", [P, E], F32), placed("page1", [P, E], F32, 14848)]
+        pages = [placed(f"page{h}", [P, E], F32, PAGES_AT + h * 4 * E) for h in range(N // P)]
         for page in pages:
-            nc.vector.memset(page[:], 0.0)
+            nc.gpsimd.memset(page[:], 0.0)
 
         gates = [sb(f"gates{u}", [P, 2, J], F32) for u in range(2)]
         larger = [sb(f"larger{u}", [P, 2, J], F32) for u in range(2)]
-        hid = [sb(f"hid{c}", [P, JP, PACK], BF16) for c in range(PARTS)]
+        hid = [sb(f"hid{c}", [P, JH, PACK], BF16) for c in range(HALVES)]
+        for t in range(PACK):
+            u, e = divmod(t, 2)
+            nc.scalar.activation(
+                out=gates[u][:, e, :], in_=gate_table[t][:].indirect(gate_list[:]),
+                func=ACT.Sigmoid, bias=offset[:, t : t + 1], scale=slope[:, t : t + 1],
+            )
+            both = psum.tile([P, 2, J], F32, name=f"both{t}")
+            w_slice = w_codes[:, t * P : (t + 1) * P].bitcast(E4M3)
+            w_plane = planes[:, W_S + t * P : W_S + (t + 1) * P]
+            nc.tensor.matmul_mx(
+                out=both[:, 0, :], lhsT=w_slice, lhsT_scale=w_plane,
+                rhs=xt_picked[:].bitcast(E2M1), rhs_scale=planes[:, XT_S : XT_S + J],
+                start=True, stop=True,
+            )
+            nc.tensor.matmul_mx(
+                out=both[:, 1, :], lhsT=w_slice, lhsT_scale=w_plane,
+                rhs=xo_picked[:].bitcast(E4M3), rhs_scale=planes[:, XO_S : XO_S + J],
+                start=True, stop=True,
+            )
+            nc.vector.tensor_reduce(
+                larger[u][:, e, :], both[:].rearrange("p s j -> p j s"), mybir.AxisListType.X, ALU.max
+            )
+
         for u in range(2):
-            for e in range(2):
-                t = 2 * u + e
-                nc.scalar.activation(
-                    out=gates[u][:, e, :], in_=gate_table[t][:].indirect(gate_list[:]),
-                    func=ACT.Sigmoid, bias=offset[:, t : t + 1], scale=slope[:, t : t + 1],
-                )
-                both = psum.tile([P, 2, J], F32, name=f"both{t}")
-                cols = slice(t * P, (t + 1) * P)
-                w_plane = planes[:, W_S + t * P : W_S + (t + 1) * P]
-                nc.tensor.matmul_mx(
-                    out=both[:, 0, :], lhsT=w_codes[:, cols].bitcast(E4M3), lhsT_scale=w_plane,
-                    rhs=xt_picked[:].bitcast(E2M1), rhs_scale=planes[:, XT_S : XT_S + J],
-                    start=True, stop=True,
-                )
-                nc.tensor.matmul_mx(
-                    out=both[:, 1, :], lhsT=w_codes[:, cols].bitcast(E4M3), lhsT_scale=w_plane,
-                    rhs=xo_picked[:].bitcast(E4M3), rhs_scale=planes[:, XO_S : XO_S + J],
-                    start=True, stop=True,
-                )
-                nc.vector.tensor_reduce(
-                    larger[u][:, e, :], both[:].rearrange("p s j -> p j s"), mybir.AxisListType.X, ALU.max
-                )
-        for u in range(2):
-            for c in range(PARTS):
-                js = slice(c * JP, (c + 1) * JP)
+            for c in range(HALVES):
+                js = slice(c * JH, (c + 1) * JH)
                 nc.vector.tensor_tensor(
                     hid[c][:, :, 2 * u : 2 * u + 2],
                     larger[u][:, :, js].rearrange("p e j -> p j e"),
@@ -167,28 +183,28 @@ def tile_list_oneforboth_tablegate_skip_scattered_kernel(
                 )
 
         sums = {}
-        for c in range(PARTS):
-            js = slice(c * JP, (c + 1) * JP)
+        for c in range(HALVES):
+            js = slice(c * JH, (c + 1) * JH)
             for h in range(N // P):
-                sums[c, h] = psum.tile([P, JP], F32, name=f"sum{c}_{h}")
+                sums[c, h] = psum.tile([P, JH], F32, name=f"sum{c}_{h}")
                 nc.tensor.matmul_mx(
                     out=sums[c, h][:], lhsT=ws_codes[:, h * P : (h + 1) * P].bitcast(E4M3),
                     lhsT_scale=planes[:, WS_S + h * P : WS_S + (h + 1) * P],
                     rhs=sx_codes[:, js].bitcast(E4M3),
-                    rhs_scale=planes[:, SX_S + c * JP : SX_S + (c + 1) * JP],
+                    rhs_scale=planes[:, SX_S + c * JH : SX_S + (c + 1) * JH],
                     start=True, stop=False,
                 )
 
-        hid_codes = [sb(f"hid_codes{c}", [P, JP], U32) for c in range(PARTS)]
-        hid_plane = [sb(f"hid_plane{c}", [P, JP], U8) for c in range(PARTS)]
-        for c in range(PARTS):
+        hid_codes = [sb(f"hid_codes{c}", [P, JH], U32) for c in range(HALVES)]
+        hid_plane = [sb(f"hid_plane{c}", [P, JH], U8) for c in range(HALVES)]
+        for c in range(HALVES):
             nc.vector.quantize_mx(
                 out=hid_codes[c][:].bitcast(E5M2), scales=hid_plane[c][:],
                 in_=hid[c][:].rearrange("p j t -> p (j t)"),
             )
 
-        for c in range(PARTS):
-            places = place_list[:, c * JP // 16 : (c + 1) * JP // 16]
+        for c in range(HALVES):
+            places = place_list[:, c * JH // GROUP : (c + 1) * JH // GROUP]
             for h in range(N // P):
                 nc.tensor.matmul_mx(
                     out=sums[c, h][:], lhsT=wb_codes[:, 2 * h * P : 2 * (h + 1) * P].bitcast(E2M1),
@@ -196,7 +212,7 @@ def tile_list_oneforboth_tablegate_skip_scattered_kernel(
                     rhs=hid_codes[c][:].bitcast(E5M2), rhs_scale=hid_plane[c][:],
                     start=False, stop=True,
                 )
-                result = sb(f"result{c}_{h}", [P, JP], F32)
+                result = sb(f"result{c}_{h}", [P, JH], F32)
                 if h == 0:
                     nc.vector.tensor_copy(result[:], sums[c, h][:])
                     nc.vector.tensor_copy(pages[h][:].indirect(places), result[:])

from contextlib import ExitStack

import concourse.mybir as mybir

K, T, Z, J, R, Q, N, L, E = 512, 1024, 1024, 256, 512, 1024, 256, 512, 1024
FLOPS = 2 * (2 * K * R * J + R * N * J + L * N * J)

F32 = mybir.dt.float32
BF16 = mybir.dt.bfloat16
I32 = mybir.dt.int32
U32 = mybir.dt.uint32
U16 = mybir.dt.uint16
U8 = mybir.dt.uint8
E4M3 = mybir.dt.float8_e4m3fn_x4
E5M2 = mybir.dt.float8_e5m2_x4
E2M1 = mybir.dt.float4_e2m1fn_x4
ACT = mybir.ActivationFunctionType
ALU = mybir.AluOpType

P = 128
PACK = 4
GROUP = 16
QUADS = 4
ROWS = 16
LOW = P - ROWS
HALVES = 2
JH = J // HALVES

XT_S, XO_S, W_S = 0, J, 2 * J
WB_S = W_S + R
SX_S = WB_S + N
WS_S = SX_S + J
W_RAW = WS_S + N
PLANE_COLS = W_RAW + R

TABLE_BYTES = 4 * Q
GATE1_AT = 0
GATE2_AT = GATE1_AT + TABLE_BYTES
WB_AT = GATE2_AT + TABLE_BYTES
GATE3_AT = WB_AT + 2 * N
XO_TABLE_AT = WB_AT - 4 * Z // 2
XT_TABLE_AT = GATE3_AT + TABLE_BYTES
PAGES_AT = XT_TABLE_AT + 2 * T
W_WORDS_AT = PAGES_AT + 4 * E - 4 * R // 2


def tile_list_oneforboth_tablegate_skip_scattered_kernel(
    tc, xt_words, xt_scales, xo_words, xo_scales, w_words, w_scales, tg, sg, bg,
    wb_words, wb_scales, sx_words, sx_scales, ws_words, ws_scales,
    offs, offs2, offs3, offs4, out,
):
    nc = tc.nc
    with ExitStack() as ctx:
        keep = ctx.enter_context(tc.tile_pool(name="keep", bufs=1))
        shared = ctx.enter_context(tc.tile_pool(name="shared", bufs=1))
        psum = ctx.enter_context(tc.psum_pool(name="psum", bufs=1))

        def sb(name, shape, dtype):
            return keep.tile(shape, dtype, name=name, align_bytes=64)

        def placed(name, shape, dtype, byte):
            return shared.tile(shape, dtype, name=name, align_bytes=64, offset=byte)

        def words(ap):
            return ap[0].rearrange("p n t -> p (n t)").bitcast(I32)

        def load_scale_rows(queue, tile, first, src):
            queue.dma_start(tile[LOW:, first : first + src.shape[2]].bitcast(I32), src[0].bitcast(I32))

        token_list = sb("token_list", [P, J // GROUP], U16)
        note_list = sb("note_list", [P, J // GROUP], U16)
        gate_list = sb("gate_list", [P, J // GROUP], U16)
        place_list = sb("place_list", [P, J // GROUP], U16)

        xt_bytes = sb("xt_bytes", [P, T], U8)
        xo_bytes = sb("xo_bytes", [P, Z], U8)
        planes = sb("planes", [P, PLANE_COLS], U8)
        xt_table = placed("xt_table", [P, T], U16, XT_TABLE_AT)
        xo_table = placed("xo_table", [P, Z], U32, XO_TABLE_AT)
        w_raw = placed("w_raw", [P, R], U32, W_WORDS_AT)
        w_codes = sb("w_codes", [P, R], U32)
        xt_picked = sb("xt_picked", [P, J], U16)
        xo_picked = sb("xo_picked", [P, J], U32)
        xt_picked_bytes = sb("xt_picked_bytes", [P, J], U8)
        xo_picked_bytes = placed("xo_picked_bytes", [P, J], U8, GATE1_AT)
        slope = sb("slope", [P, PACK], F32)
        offset = sb("offset", [P, PACK], F32)
        gate_table = [sb("gate_table0", [P, Q], F32)]

        nc.vector.memset(xt_bytes[:LOW, :].bitcast(I32), 0)
        nc.vector.memset(xo_bytes[:LOW, :].bitcast(I32), 0)
        nc.vector.memset(planes[:LOW, WB_S:].bitcast(I32), 0)

        load_scale_rows(nc.scalar, planes, W_RAW, w_scales)
        load_scale_rows(nc.scalar, planes, WB_S, wb_scales)
        nc.sync.dma_start(token_list[:], offs)
        load_scale_rows(nc.sync, xt_bytes, 0, xt_scales)
        nc.sync.dma_start(note_list[:], offs2)
        load_scale_rows(nc.sync, xo_bytes, 0, xo_scales)
        nc.sync.dma_start(xo_table[:].bitcast(I32), words(xo_words))
        nc.sync.dma_start(xt_table[:].bitcast(I32), xt_words[0].bitcast(I32))
        load_scale_rows(nc.sync, planes, SX_S, sx_scales)
        load_scale_rows(nc.sync, planes, WS_S, ws_scales)
        nc.sync.dma_start(gate_list[:], offs3)
        nc.sync.dma_start(place_list[:], offs4)
        nc.sync.dma_start(w_raw[:].bitcast(I32), words(w_words))
        tg_slices = tg.rearrange("(p t) q -> t p q", t=PACK)
        nc.sync.dma_start(gate_table[0][:], tg_slices[0])
        nc.sync.dma_start(slope[:], sg.rearrange("(p t) o -> p (t o)", t=PACK))
        nc.sync.dma_start(offset[:], bg.rearrange("(p t) o -> p (t o)", t=PACK))

        nc.vector.tensor_copy(
            planes[:, W_S : W_S + R].rearrange("p (t m) -> p t m", t=PACK),
            planes[:, W_RAW:].rearrange("p (m t) -> p t m", t=PACK),
        )
        nc.vector.tensor_copy(xt_picked_bytes[:], xt_bytes[:].indirect(token_list[:]))
        nc.vector.tensor_copy(xo_picked_bytes[:], xo_bytes[:].indirect(note_list[:]))
        nc.vector.tensor_copy(planes[:, XT_S : XT_S + J].bitcast(I32), xt_picked_bytes[:].bitcast(I32))
        nc.vector.tensor_copy(planes[:, XO_S : XO_S + J].bitcast(I32), xo_picked_bytes[:].bitcast(I32))

        for quad in range(QUADS):
            nc.sync.dma_start(
                planes[32 * quad : 32 * quad + 4, :W_RAW].bitcast(I32),
                planes[LOW + 4 * quad : LOW + 4 * quad + 4, :W_RAW].bitcast(I32),
            )

        nc.vector.tensor_copy(xo_picked[:], xo_table[:].indirect(note_list[:]))
        for t, byte in ((1, GATE1_AT), (2, GATE2_AT), (3, GATE3_AT)):
            gate_table.append(placed(f"gate_table{t}", [P, Q], F32, byte))
            nc.sync.dma_start(gate_table[t][:], tg_slices[t])

        nc.vector.tensor_copy(xt_picked[:], xt_table[:].indirect(token_list[:]))
        nc.vector.tensor_copy(
            w_codes[:].rearrange("p (t m) -> p t m", t=PACK),
            w_raw[:].rearrange("p (m t) -> p t m", t=PACK),
        )

        ws_codes = placed("ws_codes", [P, N], U32, XT_TABLE_AT)
        sx_codes = placed("sx_codes", [P, J], U32, XT_TABLE_AT + 4 * N)
        wb_codes = placed("wb_codes", [P, 2 * N], U8, WB_AT)
        nc.sync.dma_start(ws_codes[:].bitcast(I32), words(ws_words))
        nc.sync.dma_start(sx_codes[:].bitcast(I32), words(sx_words))
        nc.sync.dma_start(wb_codes[:].bitcast(I32), wb_words[0].bitcast(I32))

        pages = [placed(f"page{h}", [P, E], F32, PAGES_AT + h * 4 * E) for h in range(N // P)]
        for page in pages:
            nc.gpsimd.memset(page[:], 0.0)

        gates = [sb(f"gates{u}", [P, 2, J], F32) for u in range(2)]
        larger = [sb(f"larger{u}", [P, 2, J], F32) for u in range(2)]
        hid = [sb(f"hid{c}", [P, JH, PACK], BF16) for c in range(HALVES)]
        for t in range(PACK):
            u, e = divmod(t, 2)
            nc.scalar.activation(
                out=gates[u][:, e, :], in_=gate_table[t][:].indirect(gate_list[:]),
                func=ACT.Sigmoid, bias=offset[:, t : t + 1], scale=slope[:, t : t + 1],
            )
            both = psum.tile([P, 2, J], F32, name=f"both{t}")
            w_slice = w_codes[:, t * P : (t + 1) * P].bitcast(E4M3)
            w_plane = planes[:, W_S + t * P : W_S + (t + 1) * P]
            nc.tensor.matmul_mx(
                out=both[:, 0, :], lhsT=w_slice, lhsT_scale=w_plane,
                rhs=xt_picked[:].bitcast(E2M1), rhs_scale=planes[:, XT_S : XT_S + J],
                start=True, stop=True,
            )
            nc.tensor.matmul_mx(
                out=both[:, 1, :], lhsT=w_slice, lhsT_scale=w_plane,
                rhs=xo_picked[:].bitcast(E4M3), rhs_scale=planes[:, XO_S : XO_S + J],
                start=True, stop=True,
            )
            nc.vector.tensor_reduce(
                larger[u][:, e, :], both[:].rearrange("p s j -> p j s"), mybir.AxisListType.X, ALU.max
            )

        for u in range(2):
            for c in range(HALVES):
                js = slice(c * JH, (c + 1) * JH)
                nc.vector.tensor_tensor(
                    hid[c][:, :, 2 * u : 2 * u + 2],
                    larger[u][:, :, js].rearrange("p e j -> p j e"),
                    gates[u][:, :, js].rearrange("p e j -> p j e"),
                    ALU.mult,
                )

        sums = {}
        for c in range(HALVES):
            js = slice(c * JH, (c + 1) * JH)
            for h in range(N // P):
                sums[c, h] = psum.tile([P, JH], F32, name=f"sum{c}_{h}")
                nc.tensor.matmul_mx(
                    out=sums[c, h][:], lhsT=ws_codes[:, h * P : (h + 1) * P].bitcast(E4M3),
                    lhsT_scale=planes[:, WS_S + h * P : WS_S + (h + 1) * P],
                    rhs=sx_codes[:, js].bitcast(E4M3),
                    rhs_scale=planes[:, SX_S + c * JH : SX_S + (c + 1) * JH],
                    start=True, stop=False,
                )

        hid_codes = [sb(f"hid_codes{c}", [P, JH], U32) for c in range(HALVES)]
        hid_plane = [sb(f"hid_plane{c}", [P, JH], U8) for c in range(HALVES)]
        for c in range(HALVES):
            nc.vector.quantize_mx(
                out=hid_codes[c][:].bitcast(E5M2), scales=hid_plane[c][:],
                in_=hid[c][:].rearrange("p j t -> p (j t)"),
            )

        for c in range(HALVES):
            places = place_list[:, c * JH // GROUP : (c + 1) * JH // GROUP]
            for h in range(N // P):
                nc.tensor.matmul_mx(
                    out=sums[c, h][:], lhsT=wb_codes[:, 2 * h * P : 2 * (h + 1) * P].bitcast(E2M1),
                    lhsT_scale=planes[:, WB_S + h * P : WB_S + (h + 1) * P],
                    rhs=hid_codes[c][:].bitcast(E5M2), rhs_scale=hid_plane[c][:],
                    start=False, stop=True,
                )
                result = sb(f"result{c}_{h}", [P, JH], F32)
                if h == 0:
                    nc.vector.tensor_copy(result[:], sums[c, h][:])
                    nc.vector.tensor_copy(pages[h][:].indirect(places), result[:])
                else:
                    nc.scalar.copy(result[:], sums[c, h][:])
                    nc.scalar.activation(out=pages[h][:].indirect(places), in_=result[:], func=ACT.Copy)

        nc.sync.dma_start(out[0:P, :], pages[0][:])
        nc.scalar.dma_start(out[P : 2 * P, :], pages[1][:])
